import numpy as np
import ml_dtypes


def mxq(x, axis, fmt="e4m3"):
    dtype, down = {"e4m3": (ml_dtypes.float8_e4m3fn, 7), "e5m2": (ml_dtypes.float8_e5m2, 14)}[fmt]
    v = np.moveaxis(np.asarray(x, np.float32).astype(ml_dtypes.bfloat16).astype(np.float64), axis, -1)
    blocks = v.reshape(v.shape[:-1] + (-1, 32))
    amax = np.abs(blocks).max(-1, keepdims=True)
    byte = np.maximum(np.where(amax > 0, np.frexp(amax)[1] - 1 + 127, 0) - down, 1)
    scale = np.exp2(byte - 127.0)
    codes = (blocks / scale).astype(np.float32).astype(dtype).astype(np.float64)
    return np.moveaxis((codes * scale).reshape(v.shape), -1, axis)


WIDE = False


def mx_kscale(k):
    if not WIDE:
        return np.ones(k)
    levels = np.array([10, -10, 5, -5, 0])
    if k % 512:
        return np.exp2(np.random.permutation(np.resize(levels, k // 32))).repeat(32)
    a = np.empty((k // 512, 16))
    for p in range(k // 512):
        a[p, :8] = np.random.permutation(np.resize(levels, 8))
        for g in range(8):
            far = levels[np.abs(levels - a[p, g]) >= 10]
            a[p, g + 8] = far[np.random.randint(len(far))]
    return np.exp2(a.ravel()).repeat(32)


def f64(x):
    return np.asarray(x).astype(np.float64)


def striped8(idx):
    return np.concatenate([x.reshape(-1, 16).T for x in idx]).astype(np.uint16)


def runs(offs, k):
    lists = np.stack([offs[16 * r : 16 * r + 16].T.reshape(-1) for r in range(8)]).astype(np.int64)
    return lists[np.arange(k) % 512 // 64]


def pack_weight(w):
    k, n = w.shape
    w = f64(np.asarray(w, np.float32).astype(ml_dtypes.bfloat16)).reshape(k // 32, 32, n)
    amax = np.abs(w).max(1)
    byte = np.clip(np.where(amax > 0, np.frexp(amax)[1] - 1 + 127 - 7, 1), 1, 254)
    scaled = (w * np.exp2(127.0 - byte)[:, None, :]).reshape(k, n).astype(np.float32)
    words = np.ascontiguousarray(scaled.reshape(k // 512, 128, 4, n).transpose(0, 1, 3, 2)).astype(ml_dtypes.float8_e4m3fn).view(np.uint8)
    return words, np.ascontiguousarray(byte.astype(np.uint8).reshape(k // 512, 16, n))


def unpack_weight(words, scales):
    g, p, n, _ = words.shape
    vals = np.ascontiguousarray(words).view(ml_dtypes.float8_e4m3fn).astype(np.float64) * np.repeat(np.exp2(scales.astype(np.float64) - 127.0), 8, axis=1)[..., None]
    return vals.transpose(0, 1, 3, 2).reshape(g * 512, n)


def sigmoid(v):
    return 1.0 / (1.0 + np.exp(-np.maximum(v, -700.0)))


K, T, S, H, C = 512, 2048, 512, 512, 512


def setup_inputs():
    n = np.random.standard_normal
    s = mx_kscale(K)[:, None]
    packed_xT = pack_weight(n((K, T)) * s)
    return {
        "x_words": packed_xT[0],
        "x_scales": packed_xT[1],
        "w1": (n((K, H)) / np.sqrt(K) / s).astype(np.float32),
        "gs": (np.random.uniform(0.5, 1.5, (K, 1)) / s).astype(np.float32),
        "offs": striped8(np.random.randint(0, T, (8, S))),
        "n1": striped8(np.stack([np.random.permutation(S) for _ in range(8)])),
        "n2": striped8(np.stack([np.random.permutation(S) for _ in range(8)])),
        "cand": striped8(np.random.randint(0, T, (8, C))),
        "n3": striped8(np.stack([np.random.permutation(S) for _ in range(8)])),
        "n4": striped8(np.stack([np.random.permutation(S) for _ in range(8)])),
    }


def reference(x_words, x_scales, w1, gs, offs, n1, n2, cand, n3, n4):
    x_cand = unpack_weight(x_words, x_scales)[np.arange(K)[:, None], runs(cand, K)]
    xq = unpack_weight(x_words, x_scales)[np.arange(K)[:, None], runs(offs, K)]
    y = mxq(f64(w1), 0, "e4m3").T @ xq
    pa = y[np.arange(H)[:, None], runs(n1, H)]
    pb = y[np.arange(H)[:, None], runs(n2, H)]
    z = f64(gs) * (np.maximum(np.maximum(y, pa), pb) - (0.5 * (np.minimum(np.minimum(y, pa), pb))))
    s = 0.0625 * ((x_cand.T @ mxq(z, 0, "e4m3")))
    st = s[np.arange(C)[:, None], runs(n3, C)] - s
    return s * (sigmoid(st[np.arange(C)[:, None], runs(n4, C)]))

@@ -1,0 +1,222 @@
+from contextlib import ExitStack
+
+import concourse.mybir as mybir
+
+K, T, S, H, C = 512, 2048, 512, 512, 512
+FLOPS = 2 * K * H * S + 2 * K * C * S
+
+F32 = mybir.dt.float32
+BF16 = mybir.dt.bfloat16
+I32 = mybir.dt.int32
+U32 = mybir.dt.uint32
+U16 = mybir.dt.uint16
+U8 = mybir.dt.uint8
+FP8X4 = mybir.dt.float8_e4m3fn_x4
+ALU = mybir.AluOpType
+ACT = mybir.ActivationFunctionType
+
+P = 128
+PACK = 4
+PIECES = ((0, 256), (256, 384), (384, 512))
+HALVES = ((0, 256), (256, 512))
+
+
+def tile_picked_hcandrangehopd_none_p_kernel(tc, x_words, x_scales, w1, gs, offs, n1, n2, cand, n3, n4, out):
+    nc = tc.nc
+    with ExitStack() as ctx:
+        held = ctx.enter_context(tc.tile_pool(name="held", bufs=1))
+        work = ctx.enter_context(tc.tile_pool(name="work", bufs=3))
+        psum = ctx.enter_context(tc.psum_pool(name="psum", bufs=1))
+
+        def load_list(name, src):
+            lst = held.tile([P, S // 16], U16, name=name)
+            nc.sync.dma_start(lst[:], src)
+            return lst
+
+        def entries(lst, a, b):
+            return lst[:, a // 16 : b // 16]
+
+        offs_l = load_list("offs_l", offs)
+        table_scales = held.tile([P, T], U8, name="table_scales", align_bytes=64)
+        nc.sync.dma_start(table_scales[:].bitcast(I32), x_scales[0].bitcast(I32).unsqueeze(1).broadcast_to([16, 8, T // 4]))
+        cand_l = load_list("cand_l", cand)
+        n1_l = load_list("n1_l", n1)
+        n2_l = load_list("n2_l", n2)
+        n3_l = load_list("n3_l", n3)
+        n4_l = load_list("n4_l", n4)
+        table_words = held.tile([P, T], U32, name="table_words", align_bytes=64)
+        nc.sync.dma_start(table_words[:].bitcast(I32), x_words[0].rearrange("p c r -> p (c r)").bitcast(I32))
+        w_raw = []
+        for h, (a, b) in enumerate(HALVES):
+            half = held.tile([P, PACK, b - a], F32, name=f"w_raw{h}")
+            nc.sync.dma_start(half[:], w1.rearrange("(p j) c -> p j c", j=PACK)[:, :, a:b])
+            w_raw.append(half)
+        gain = held.tile([P, PACK], F32, name="gain")
+        nc.gpsimd.dma_start(gain[:], gs.rearrange("(p t) o -> p (t o)", t=PACK))
+
+        x_plane = held.tile([P, S], U8, name="x_plane", align_bytes=64)
+        c_plane = held.tile([P, C], U8, name="c_plane", align_bytes=64)
+        nc.vector.memset(x_plane[:].bitcast(I32), 0)
+        nc.vector.memset(c_plane[:].bitcast(I32), 0)
+
+        x_bytes = held.tile([P, S], U8, name="x_bytes", align_bytes=64)
+        nc.vector.tensor_copy(x_bytes[:], table_scales[:].indirect(offs_l[:]))
+        for r in range(4):
+            nc.scalar.dma_start(x_plane[r:P:32, :].bitcast(I32), x_bytes[8 * r : P : 32, :].bitcast(I32))
+        c_bytes = held.tile([P, C], U8, name="c_bytes", align_bytes=64)
+        nc.vector.tensor_copy(c_bytes[:], table_scales[:].indirect(cand_l[:]))
+
+        gain_half = held.tile([P, PACK], F32, name="gain_half")
+        gain_neg_half = held.tile([P, PACK], F32, name="gain_neg_half")
+        nc.gpsimd.tensor_scalar(gain_half[:], gain[:], 0.5, 0.0, ALU.mult, ALU.add)
+        nc.gpsimd.tensor_scalar(gain_neg_half[:], gain[:], -0.5, 0.0, ALU.mult, ALU.add)
+
+        c_bytes_dealt = held.tile([P, C], U8, name="c_bytes_dealt", align_bytes=64)
+        nc.vector.tensor_copy(
+            c_bytes_dealt[:].bitcast(I32).rearrange("p (t a b) -> p t a b", t=PACK, b=2),
+            c_bytes[:].bitcast(I32).rearrange("p (a t b) -> p t a b", t=PACK, b=2),
+        )
+        for r in range(4):
+            nc.sync.dma_start(c_plane[r:P:32, :].bitcast(I32), c_bytes_dealt[8 * r : P : 32, :].bitcast(I32))
+
+        x_codes = held.tile([P, S], U32, name="x_codes", align_bytes=64)
+        nc.vector.tensor_copy(x_codes[:], table_words[:].indirect(offs_l[:]))
+        c_words = held.tile([P, C], U32, name="c_words", align_bytes=64)
+        nc.vector.tensor_copy(c_words[:], table_words[:].indirect(cand_l[:]))
+        c_codes = held.tile([P, C], U32, name="c_codes", align_bytes=64)
+        nc.vector.tensor_copy(
+            c_codes[:].rearrange("p (t a b) -> p t a b", t=PACK, b=8),
+            c_words[:].rearrange("p (a t b) -> p t a b", t=PACK, b=8),
+        )
+
+        w_bf = held.tile([P, H * PACK], BF16, name="w_bf", align_bytes=64)
+        w_view = w_bf[:].rearrange("p (t m j) -> p m j t", t=PACK, j=PACK)
+        w_src = [w_raw[h][:].rearrange("p j (m t) -> p m j t", t=PACK) for h in range(2)]
+        nc.scalar.copy(w_view[:, 0:64], w_src[0])
+        nc.vector.tensor_copy(w_view[:, 64:128, :, 0:2], w_src[1][:, :, :, 0:2])
+        nc.scalar.copy(w_view[:, 64:128, :, 2:4], w_src[1][:, :, :, 2:4])
+        w_codes = held.tile([P, H], U32, name="w_codes", align_bytes=64)
+        w_plane = held.tile([P, H], U8, name="w_plane", align_bytes=64)
+        for a, b in HALVES:
+            nc.vector.quantize_mx(out=w_codes[:, a:b].bitcast(FP8X4), scales=w_plane[:, a:b], in_=w_bf[:, a * PACK : b * PACK])
+
+        y_win = []
+        y_banks = []
+        y_plain = held.tile([P, PACK, S], F32, name="y_plain")
+        y_gain = held.tile([P, PACK, S], F32, name="y_gain")
+        for t in range(PACK):
+            bank = psum.tile([P, S], F32, name=f"y_bank{t}")
+            cols = slice(t * P, (t + 1) * P)
+            nc.tensor.matmul_mx(out=bank[:], lhsT=w_codes[:, cols].bitcast(FP8X4), lhsT_scale=w_plane[:, cols],
+                                rhs=x_codes[:].bitcast(FP8X4), rhs_scale=x_plane[:], start=True, stop=True)
+            win = held.tile([P, S], F32, name=f"y_win{t}")
+            nc.scalar.copy(win[:], bank[:])
+            y_win.append(win)
+            y_banks.append(bank)
+            a, b = HALVES[0]
+            nc.scalar.copy(y_plain[:, t, a:b], bank[:, a:b])
+            nc.scalar.activation(y_gain[:, t, a:b], bank[:, a:b], ACT.Copy, scale=gain_half[:, t : t + 1])
+        a, b = HALVES[1]
+        for t in range(PACK):
+            nc.scalar.copy(y_plain[:, t, a:b], y_banks[t][:, a:b])
+            nc.scalar.activation(y_gain[:, t, a:b], y_banks[t][:, a:b], ACT.Copy, scale=gain_half[:, t : t + 1])
+
+        z_codes = held.tile([P, S], U32, name="z_codes", align_bytes=64)
+        z_plane = held.tile([P, S], U8, name="z_plane", align_bytes=64)
+        s_banks = [psum.tile([P, S], F32, name=f"s_bank{t}") for t in range(PACK)]
+        s_win = [held.tile([P, S], F32, name=f"s_win{t}") for t in range(PACK)]
+        s_plain = [held.tile([P, S], F32, name=f"s_plain{t}") for t in range(PACK)]
+        z_rows = [held.tile([P, PACK, b - a], F32, name=f"z_rows{i}") for i, (a, b) in enumerate(PIECES)]
+        state = {}
+
+        def fetch(u, which):
+            i, t = u
+            a, b = PIECES[i]
+            d = work.tile([P, b - a], F32, name=f"diff{which}")
+            lst = (n1_l, n2_l)[which]
+            nc.vector.tensor_tensor(d[:], y_win[t][:].indirect(entries(lst, a, b)), y_plain[:, t, a:b], ALU.subtract)
+            state[u, "d", which] = d
+
+        def extremes(u):
+            i, t = u
+            a, b = PIECES[i]
+            hi = work.tile([P, b - a], F32, name="hi")
+            lo = work.tile([P, b - a], F32, name="lo")
+            d0, d1 = state[u, "d", 0], state[u, "d", 1]
+            nc.vector.scalar_tensor_tensor(lo[:], d0[:], 0.0, d1[:], ALU.min, ALU.min)
+            nc.vector.scalar_tensor_tensor(hi[:], d0[:], 0.0, d1[:], ALU.max, ALU.max)
+            state[u, "hi"], state[u, "lo"] = hi, lo
+
+        def low_part(u):
+            i, t = u
+            a, b = PIECES[i]
+            part = work.tile([P, b - a], F32, name="part")
+            nc.vector.scalar_tensor_tensor(part[:], state[u, "lo"][:], gain_neg_half[:, t : t + 1], y_gain[:, t, a:b], ALU.mult, ALU.add)
+            state[u, "part"] = part
+
+        def finish(u):
+            i, t = u
+            nc.vector.scalar_tensor_tensor(z_rows[i][:, t, :], state[u, "hi"][:], gain[:, t : t + 1], state[u, "part"][:], ALU.mult, ALU.add)
+
+        def interleave(i):
+            a, b = PIECES[i]
+            z_bf = held.tile([P, (b - a) * PACK], BF16, name=f"z_bf{i}", align_bytes=64)
+            dst = z_bf[:].rearrange("p (c i t) -> p c t i", i=4, t=PACK)
+            src = z_rows[i][:].rearrange("p t (c i) -> p c t i", i=4)
+            if i == len(PIECES) - 1:
+                nc.vector.tensor_copy(dst, src)
+            else:
+                nc.scalar.copy(dst, src)
+            state[i, "z_bf"] = z_bf
+
+        def score(i):
+            a, b = PIECES[i]
+            nc.vector.quantize_mx(out=z_codes[:, a:b].bitcast(FP8X4), scales=z_plane[:, a:b], in_=state[i, "z_bf"][:])
+            for t in range(PACK):
+                cols = slice(t * P, (t + 1) * P)
+                nc.tensor.matmul_mx(out=s_banks[t][:, a:b], lhsT=c_codes[:, cols].bitcast(FP8X4), lhsT_scale=c_plane[:, cols],
+                                    rhs=z_codes[:, a:b].bitcast(FP8X4), rhs_scale=z_plane[:, a:b], start=True, stop=True)
+                nc.scalar.activation(s_win[t][:, a:b], s_banks[t][:, a:b], ACT.Copy, scale=0.0625)
+                nc.scalar.activation(s_plain[t][:, a:b], s_banks[t][:, a:b], ACT.Copy, scale=0.0625)
+
+        units = [(i, t) for i in range(len(PIECES)) for t in range(PACK)]
+        for n in range(len(units) + 2):
+            if n < len(units):
+                fetch(units[n], 0)
+            if n >= 2:
+                finish(units[n - 2])
+                if units[n - 2][1] == PACK - 1:
+                    interleave(units[n - 2][0])
+            if 1 <= n <= len(units):
+                extremes(units[n - 1])
+            if n < len(units):
+                fetch(units[n], 1)
+            if 1 <= n <= len(units):
+                low_part(units[n - 1])
+            if n >= 3 and units[n - 3][1] == PACK - 1:
+                score(units[n - 3][0])
+        score(len(PIECES) - 1)
+
+        out_rows = out.rearrange("(a t b) j -> t a b j", t=PACK, b=8)
+        gates = {}
+
+        def step(t):
+            st = work.tile([P, S], F32, name="st")
+            for a, b in HALVES:
+                nc.vector.tensor_tensor(st[:, a:b], s_win[t][:].indirect(entries(n3_l, a, b)), s_plain[t][:, a:b], ALU.subtract)
+            for a, b in HALVES:
+                gate = work.tile([P, b - a], F32, name="gate", bufs=4)
+                nc.scalar.activation(gate[:], st[:].indirect(entries(n4_l, a, b)), ACT.Sigmoid)
+                gates[t, a] = gate
+
+        def emit(t):
+            for a, b in HALVES:
+                res = work.tile([P, b - a], F32, name="res", bufs=8)
+                nc.vector.tensor_tensor(res[:], gates[t, a][:], s_plain[t][:, a:b], ALU.mult)
+                nc.sync.dma_start(out_rows[t][:, :, a:b], res[:])
+
+        for t in range(PACK + 1):
+            if t < PACK:
+                step(t)
+            if t >= 1:
+                emit(t - 1)

@@ -1,6 +1,8 @@
 from contextlib import ExitStack
+from functools import partial
 
 import concourse.mybir as mybir
+from concourse.masks import make_identity
 
 K, T, S, H, C = 512, 2048, 512, 512, 512
 FLOPS = 2 * K * H * S + 2 * K * C * S
@@ -36,23 +38,42 @@ def tile_picked_hcandrangehopd_none_p_kernel(tc, x_words, x_scales, w1, gs, offs
         def entries(lst, a, b):
             return lst[:, a // 16 : b // 16]
 
+        warm_in = held.tile([P, 1], F32, name="warm_in")
+        warm_out = held.tile([P, 1], F32, name="warm_out")
+        nc.gpsimd.memset(warm_in[:], 0.0)
+        nc.scalar.activation(warm_out[:], warm_in[:], ACT.Sigmoid)
+
         offs_l = load_list("offs_l", offs)
         table_scales = held.tile([P, T], U8, name="table_scales", align_bytes=64)
         nc.sync.dma_start(table_scales[:].bitcast(I32), x_scales[0].bitcast(I32).unsqueeze(1).broadcast_to([16, 8, T // 4]))
         cand_l = load_list("cand_l", cand)
         n1_l = load_list("n1_l", n1)
         n2_l = load_list("n2_l", n2)
-        n3_l = load_list("n3_l", n3)
-        n4_l = load_list("n4_l", n4)
         table_words = held.tile([P, T], U32, name="table_words", align_bytes=64)
-        nc.sync.dma_start(table_words[:].bitcast(I32), x_words[0].rearrange("p c r -> p (c r)").bitcast(I32))
+        words_src = x_words[0].rearrange("p c r -> p (c r)").bitcast(I32)
+        for h in range(2):
+            cols = slice(h * T // 2, (h + 1) * T // 2)
+            nc.sync.dma_start(table_words[:].bitcast(I32)[:, cols], words_src[:, cols])
         w_raw = []
         for h, (a, b) in enumerate(HALVES):
             half = held.tile([P, PACK, b - a], F32, name=f"w_raw{h}")
             nc.sync.dma_start(half[:], w1.rearrange("(p j) c -> p j c", j=PACK)[:, :, a:b])
             w_raw.append(half)
+        n3_l = load_list("n3_l", n3)
+        n4_l = load_list("n4_l", n4)
         gain = held.tile([P, PACK], F32, name="gain")
         nc.gpsimd.dma_start(gain[:], gs.rearrange("(p t) o -> p (t o)", t=PACK))
+
+        gain_half = held.tile([P, PACK], F32, name="gain_half")
+        sign3 = held.tile([P, PACK], F32, name="sign3")
+        top_factor = held.tile([P, PACK], F32, name="top_factor")
+        low_factor = held.tile([P, PACK], F32, name="low_factor")
+        nc.gpsimd.tensor_scalar(gain_half[:], gain[:], 0.5, 0.0, ALU.mult, ALU.add)
+        nc.gpsimd.tensor_scalar(sign3[:], gain[:], 0.0, 3.0, ALU.is_ge, ALU.mult)
+        nc.gpsimd.tensor_scalar(top_factor[:], sign3[:], 1.0, -1.0, ALU.mult, ALU.add)
+        nc.gpsimd.tensor_scalar(low_factor[:], sign3[:], -1.0, 2.0, ALU.mult, ALU.add)
+        ident = held.tile([P, P], F32, name="ident")
+        make_identity(nc, ident[:])
 
         x_plane = held.tile([P, S], U8, name="x_plane", align_bytes=64)
         c_plane = held.tile([P, C], U8, name="c_plane", align_bytes=64)
@@ -66,11 +87,6 @@ def tile_picked_hcandrangehopd_none_p_kernel(tc, x_words, x_scales, w1, gs, offs
         c_bytes = held.tile([P, C], U8, name="c_bytes", align_bytes=64)
         nc.vector.tensor_copy(c_bytes[:], table_scales[:].indirect(cand_l[:]))
 
-        gain_half = held.tile([P, PACK], F32, name="gain_half")
-        gain_neg_half = held.tile([P, PACK], F32, name="gain_neg_half")
-        nc.gpsimd.tensor_scalar(gain_half[:], gain[:], 0.5, 0.0, ALU.mult, ALU.add)
-        nc.gpsimd.tensor_scalar(gain_neg_half[:], gain[:], -0.5, 0.0, ALU.mult, ALU.add)
-
         c_bytes_dealt = held.tile([P, C], U8, name="c_bytes_dealt", align_bytes=64)
         nc.vector.tensor_copy(
             c_bytes_dealt[:].bitcast(I32).rearrange("p (t a b) -> p t a b", t=PACK, b=2),
@@ -81,7 +97,23 @@ def tile_picked_hcandrangehopd_none_p_kernel(tc, x_words, x_scales, w1, gs, offs
 
         x_codes = held.tile([P, S], U32, name="x_codes", align_bytes=64)
         nc.vector.tensor_copy(x_codes[:], table_words[:].indirect(offs_l[:]))
-        c_words = held.tile([P, C], U32, name="c_words", align_bytes=64)
+
+        w_first = held.tile([P, P * PACK], BF16, name="w_first", tag="w_first", align_bytes=64)
+        w_rest = held.tile([P, (H - P) * PACK], BF16, name="w_rest", align_bytes=64)
+        first_view = w_first[:].rearrange("p (m j) -> p m j", j=PACK)
+        rest_view = w_rest[:].rearrange("p (t m j) -> p m j t", t=PACK - 1, j=PACK)
+        w_src = [w_raw[h][:].rearrange("p j (m t) -> p m j t", t=PACK) for h in range(2)]
+        nc.scalar.copy(first_view[:, 0:64], w_src[0][:, :, :, 0])
+        nc.scalar.copy(rest_view[:, 0:64], w_src[0][:, :, :, 1:4])
+        nc.vector.tensor_copy(first_view[:, 64:128], w_src[1][:, :, :, 0])
+        nc.scalar.copy(rest_view[:, 64:128], w_src[1][:, :, :, 1:4])
+        w_codes = held.tile([P, H], U32, name="w_codes", align_bytes=64)
+        w_plane = held.tile([P, H], U8, name="w_plane", align_bytes=64)
+        nc.vector.quantize_mx(out=w_codes[:, 0:P].bitcast(FP8X4), scales=w_plane[:, 0:P], in_=w_first[:])
+        for a, b in ((128, 256), (256, 512)):
+            nc.vector.quantize_mx(out=w_codes[:, a:b].bitcast(FP8X4), scales=w_plane[:, a:b], in_=w_rest[:, (a - P) * PACK : (b - P) * PACK])
+
+        c_words = held.tile([P, C], U32, name="c_words", tag="w_first", align_bytes=64)
         nc.vector.tensor_copy(c_words[:], table_words[:].indirect(cand_l[:]))
         c_codes = held.tile([P, C], U32, name="c_codes", align_bytes=64)
         nc.vector.tensor_copy(
@@ -89,134 +121,143 @@ def tile_picked_hcandrangehopd_none_p_kernel(tc, x_words, x_scales, w1, gs, offs
             c_words[:].rearrange("p (a t b) -> p t a b", t=PACK, b=8),
         )
 
-        w_bf = held.tile([P, H * PACK], BF16, name="w_bf", align_bytes=64)
-        w_view = w_bf[:].rearrange("p (t m j) -> p m j t", t=PACK, j=PACK)
-        w_src = [w_raw[h][:].rearrange("p j (m t) -> p m j t", t=PACK) for h in range(2)]
-        nc.scalar.copy(w_view[:, 0:64], w_src[0])
-        nc.vector.tensor_copy(w_view[:, 64:128, :, 0:2], w_src[1][:, :, :, 0:2])
-        nc.scalar.copy(w_view[:, 64:128, :, 2:4], w_src[1][:, :, :, 2:4])
-        w_codes = held.tile([P, H], U32, name="w_codes", align_bytes=64)
-        w_plane = held.tile([P, H], U8, name="w_plane", align_bytes=64)
-        for a, b in HALVES:
-            nc.vector.quantize_mx(out=w_codes[:, a:b].bitcast(FP8X4), scales=w_plane[:, a:b], in_=w_bf[:, a * PACK : b * PACK])
-
-        y_win = []
-        y_banks = []
+        y_win = [held.tile([P, S], F32, name=f"y_win{t}") for t in range(PACK)]
         y_plain = held.tile([P, PACK, S], F32, name="y_plain")
-        y_gain = held.tile([P, PACK, S], F32, name="y_gain")
         for t in range(PACK):
-            bank = psum.tile([P, S], F32, name=f"y_bank{t}")
             cols = slice(t * P, (t + 1) * P)
+            bank = psum.tile([P, S], F32, name=f"y_bank{t}", tag=f"bank{t}")
             nc.tensor.matmul_mx(out=bank[:], lhsT=w_codes[:, cols].bitcast(FP8X4), lhsT_scale=w_plane[:, cols],
                                 rhs=x_codes[:].bitcast(FP8X4), rhs_scale=x_plane[:], start=True, stop=True)
-            win = held.tile([P, S], F32, name=f"y_win{t}")
-            nc.scalar.copy(win[:], bank[:])
-            y_win.append(win)
-            y_banks.append(bank)
-            a, b = HALVES[0]
-            nc.scalar.copy(y_plain[:, t, a:b], bank[:, a:b])
-            nc.scalar.activation(y_gain[:, t, a:b], bank[:, a:b], ACT.Copy, scale=gain_half[:, t : t + 1])
-        a, b = HALVES[1]
-        for t in range(PACK):
-            nc.scalar.copy(y_plain[:, t, a:b], y_banks[t][:, a:b])
-            nc.scalar.activation(y_gain[:, t, a:b], y_banks[t][:, a:b], ACT.Copy, scale=gain_half[:, t : t + 1])
+            nc.scalar.activation(y_win[t][:], bank[:], ACT.Copy, scale=gain_half[:, t : t + 1])
+            nc.scalar.activation(y_plain[:, t, 0:256], bank[:, 0:256], ACT.Copy, scale=gain_half[:, t : t + 1])
+            nc.sync.dma_start(y_plain[:, t, 256:512], y_win[t][:, 256:512])
 
         z_codes = held.tile([P, S], U32, name="z_codes", align_bytes=64)
         z_plane = held.tile([P, S], U8, name="z_plane", align_bytes=64)
-        s_banks = [psum.tile([P, S], F32, name=f"s_bank{t}") for t in range(PACK)]
+        s_banks = [psum.tile([P, S], F32, name=f"s_bank{t}", tag=f"bank{4 + t}") for t in range(PACK)]
         s_win = [held.tile([P, S], F32, name=f"s_win{t}") for t in range(PACK)]
         s_plain = [held.tile([P, S], F32, name=f"s_plain{t}") for t in range(PACK)]
-        z_rows = [held.tile([P, PACK, b - a], F32, name=f"z_rows{i}") for i, (a, b) in enumerate(PIECES)]
+        z_bf = [held.tile([P, b - a, PACK], BF16, name=f"z_bf{i}", align_bytes=64) for i, (a, b) in enumerate(PIECES)]
+        z_rows = held.tile([P, PACK, P], F32, name="z_rows")
+        sums = [psum.tile([P, PACK, P], F32, name=f"sum{blk}", tag=f"bank{blk}") for blk in range(3)]
+        units = [(i, t0, t0 + 2) for i in range(len(PIECES)) for t0 in (0, 2)]
+        last = len(PIECES) - 1
         state = {}
 
-        def fetch(u, which):
-            i, t = u
+        def fresh(u, name):
+            i, t0, t1 = u
             a, b = PIECES[i]
-            d = work.tile([P, b - a], F32, name=f"diff{which}")
-            lst = (n1_l, n2_l)[which]
-            nc.vector.tensor_tensor(d[:], y_win[t][:].indirect(entries(lst, a, b)), y_plain[:, t, a:b], ALU.subtract)
-            state[u, "d", which] = d
+            state[u, name] = work.tile([P, t1 - t0, b - a], F32, name=name)
+            return state[u, name]
 
-        def extremes(u):
-            i, t = u
+        def fetches(u):
+            i, t0, t1 = u
             a, b = PIECES[i]
-            hi = work.tile([P, b - a], F32, name="hi")
-            lo = work.tile([P, b - a], F32, name="lo")
-            d0, d1 = state[u, "d", 0], state[u, "d", 1]
-            nc.vector.scalar_tensor_tensor(lo[:], d0[:], 0.0, d1[:], ALU.min, ALU.min)
-            nc.vector.scalar_tensor_tensor(hi[:], d0[:], 0.0, d1[:], ALU.max, ALU.max)
-            state[u, "hi"], state[u, "lo"] = hi, lo
+            da, db = fresh(u, "da"), fresh(u, "db")
 
-        def low_part(u):
-            i, t = u
+            def fetch(d, lst, t):
+                nc.vector.tensor_tensor(d[:, t - t0, :], y_win[t][:].indirect(entries(lst, a, b)), y_plain[:, t, a:b], ALU.subtract)
+
+            return [partial(fetch, d, lst, t) for t in range(t0, t1) for d, lst in ((da, n1_l), (db, n2_l))]
+
+        def turn_back(i, blk):
             a, b = PIECES[i]
-            part = work.tile([P, b - a], F32, name="part")
-            nc.vector.scalar_tensor_tensor(part[:], state[u, "lo"][:], gain_neg_half[:, t : t + 1], y_gain[:, t, a:b], ALU.mult, ALU.add)
-            state[u, "part"] = part
+            turned = work.tile([P, 2, P, 2], BF16, name="turned")
+            nc.scalar.copy(turned[:], sums[blk][:].rearrange("j (u e) p -> j u p e", e=2))
+            words = turned[:].rearrange("j u p e -> j u (p e)").bitcast(F32)
+            back = psum.tile([P, 2, P], F32, name="back", tag="bank3")
+            for u in range(2):
+                nc.tensor.transpose(back[:, u, :], words[:, u, :], ident[:])
+            c0 = blk * P - a
+            dst = z_bf[i][:, c0 : c0 + P, :].rearrange("p c t -> p (c t)").bitcast(F32).rearrange("p (c u) -> p c u", u=2)
+            nc.scalar.copy(dst, back[:].rearrange("p u c -> p c u"))
 
-        def finish(u):
-            i, t = u
-            nc.vector.scalar_tensor_tensor(z_rows[i][:, t, :], state[u, "hi"][:], gain[:, t : t + 1], state[u, "part"][:], ALU.mult, ALU.add)
-
-        def interleave(i):
+        def combines(u):
+            i, t0, t1 = u
             a, b = PIECES[i]
-            z_bf = held.tile([P, (b - a) * PACK], BF16, name=f"z_bf{i}", align_bytes=64)
-            dst = z_bf[:].rearrange("p (c i t) -> p c t i", i=4, t=PACK)
-            src = z_rows[i][:].rearrange("p t (c i) -> p c t i", i=4)
-            if i == len(PIECES) - 1:
-                nc.vector.tensor_copy(dst, src)
-            else:
-                nc.scalar.copy(dst, src)
-            state[i, "z_bf"] = z_bf
+
+            def extremes():
+                da, db = state[u, "da"], state[u, "db"]
+                nc.vector.scalar_tensor_tensor(fresh(u, "low")[:], da[:], 0.0, db[:], ALU.min, ALU.min)
+                nc.vector.scalar_tensor_tensor(fresh(u, "top")[:], da[:], 0.0, db[:], ALU.max, ALU.max)
+
+            def by_tensor():
+                low_s, top_s = fresh(u, "low_s"), fresh(u, "top_s")
+                for t in range(t0, t1):
+                    q = t - t0
+                    nc.scalar.activation(low_s[:, q, :], state[u, "low"][:, q, :], ACT.Copy, scale=low_factor[:, t : t + 1])
+                    nc.scalar.activation(top_s[:, q, :], state[u, "top"][:, q, :], ACT.Copy, scale=top_factor[:, t : t + 1])
+                    for blk in range(a // P, b // P):
+                        c0 = blk * P - a
+                        terms = (y_plain[:, t, blk * P : (blk + 1) * P], low_s[:, q, c0 : c0 + P], top_s[:, q, c0 : c0 + P])
+                        for k, term in enumerate(terms):
+                            nc.tensor.matmul(sums[blk][:, t, :], term, ident[:], start=k == 0, stop=k == 2, is_transpose=True)
+                if t1 == PACK:
+                    for blk in range(a // P, b // P):
+                        turn_back(i, blk)
+
+            def low_part():
+                part = fresh(u, "part")
+                for t in range(t0, t1):
+                    nc.vector.scalar_tensor_tensor(part[:, t - t0, :], state[u, "low"][:, t - t0, :], low_factor[:, t : t + 1], y_plain[:, t, a:b], ALU.mult, ALU.add)
+
+            def top_part():
+                for t in range(t0, t1):
+                    nc.vector.scalar_tensor_tensor(z_rows[:, t, :], state[u, "top"][:, t - t0, :], top_factor[:, t : t + 1], state[u, "part"][:, t - t0, :], ALU.mult, ALU.add)
+
+            return [extremes, low_part, top_part] if i == last else [extremes, by_tensor]
 
         def score(i):
             a, b = PIECES[i]
-            nc.vector.quantize_mx(out=z_codes[:, a:b].bitcast(FP8X4), scales=z_plane[:, a:b], in_=state[i, "z_bf"][:])
+            nc.vector.quantize_mx(out=z_codes[:, a:b].bitcast(FP8X4), scales=z_plane[:, a:b], in_=z_bf[i][:].rearrange("p c t -> p (c t)"))
             for t in range(PACK):
                 cols = slice(t * P, (t + 1) * P)
                 nc.tensor.matmul_mx(out=s_banks[t][:, a:b], lhsT=c_codes[:, cols].bitcast(FP8X4), lhsT_scale=c_plane[:, cols],
                                     rhs=z_codes[:, a:b].bitcast(FP8X4), rhs_scale=z_plane[:, a:b], start=True, stop=True)
                 nc.scalar.activation(s_win[t][:, a:b], s_banks[t][:, a:b], ACT.Copy, scale=0.0625)
-                nc.scalar.activation(s_plain[t][:, a:b], s_banks[t][:, a:b], ACT.Copy, scale=0.0625)
+                if i > 0:
+                    nc.scalar.activation(s_plain[t][:, a:b], s_banks[t][:, a:b], ACT.Copy, scale=0.0625)
+                else:
+                    nc.sync.dma_start(s_plain[t][:, a:b], s_win[t][:, a:b])
 
-        units = [(i, t) for i in range(len(PIECES)) for t in range(PACK)]
-        for n in range(len(units) + 2):
-            if n < len(units):
-                fetch(units[n], 0)
-            if n >= 2:
-                finish(units[n - 2])
-                if units[n - 2][1] == PACK - 1:
-                    interleave(units[n - 2][0])
-            if 1 <= n <= len(units):
-                extremes(units[n - 1])
-            if n < len(units):
-                fetch(units[n], 1)
-            if 1 <= n <= len(units):
-                low_part(units[n - 1])
-            if n >= 3 and units[n - 3][1] == PACK - 1:
-                score(units[n - 3][0])
-        score(len(PIECES) - 1)
+        score_after = {4: 0, 5: 1}
+        for n in range(len(units) + 1):
+            ahead = fetches(units[n]) if n < len(units) else []
+            behind = combines(units[n - 1]) if n >= 1 else []
+            for k in range(max(len(ahead), len(behind))):
+                if k < len(ahead):
+                    ahead[k]()
+                if k < len(behind):
+                    behind[k]()
+            if n in score_after:
+                score(score_after[n])
+        nc.vector.tensor_copy(
+            z_bf[last][:].rearrange("p (c i) t -> p c t i", i=4),
+            z_rows[:].rearrange("p t (c i) -> p c t i", i=4),
+        )
+        score(last)
 
         out_rows = out.rearrange("(a t b) j -> t a b j", t=PACK, b=8)
         gates = {}
 
+        last_parts = ((0, 256), (256, 384), (384, 512))
+
         def step(t):
-            st = work.tile([P, S], F32, name="st")
+            st = work.tile([P, S], F32, name="st", bufs=4)
             for a, b in HALVES:
                 nc.vector.tensor_tensor(st[:, a:b], s_win[t][:].indirect(entries(n3_l, a, b)), s_plain[t][:, a:b], ALU.subtract)
-            for a, b in HALVES:
-                gate = work.tile([P, b - a], F32, name="gate", bufs=4)
-                nc.scalar.activation(gate[:], st[:].indirect(entries(n4_l, a, b)), ACT.Sigmoid)
-                gates[t, a] = gate
+            gates[t] = work.tile([P, S], F32, name="gate", bufs=4)
+            for a, b in last_parts if t == PACK - 1 else HALVES:
+                nc.scalar.activation(gates[t][:, a:b], st[:].indirect(entries(n4_l, a, b)), ACT.Sigmoid)
 
         def emit(t):
-            for a, b in HALVES:
-                res = work.tile([P, b - a], F32, name="res", bufs=8)
-                nc.vector.tensor_tensor(res[:], gates[t, a][:], s_plain[t][:, a:b], ALU.mult)
+            for a, b in last_parts if t == PACK - 1 else ((0, S),):
+                res = work.tile([P, b - a], F32, name="res", bufs=6)
+                nc.vector.tensor_tensor(res[:], gates[t][:, a:b], s_plain[t][:, a:b], ALU.mult)
                 nc.sync.dma_start(out_rows[t][:, :, a:b], res[:])
 
-        for t in range(PACK + 1):
+        for t in range(PACK + 2):
             if t < PACK:
                 step(t)
-            if t >= 1:
-                emit(t - 1)
+            if t >= 2:
+                emit(t - 2)

@@ -68,10 +68,10 @@ def tile_picked_hcandrangehopd_none_p_kernel(tc, x_words, x_scales, w1, gs, offs
         sign3 = held.tile([P, PACK], F32, name="sign3")
         top_factor = held.tile([P, PACK], F32, name="top_factor")
         low_factor = held.tile([P, PACK], F32, name="low_factor")
-        nc.gpsimd.tensor_scalar(gain_half[:], gain[:], 0.5, 0.0, ALU.mult, ALU.add)
-        nc.gpsimd.tensor_scalar(sign3[:], gain[:], 0.0, 3.0, ALU.is_ge, ALU.mult)
-        nc.gpsimd.tensor_scalar(top_factor[:], sign3[:], 1.0, -1.0, ALU.mult, ALU.add)
-        nc.gpsimd.tensor_scalar(low_factor[:], sign3[:], -1.0, 2.0, ALU.mult, ALU.add)
+        nc.scalar.activation(gain_half[:], gain[:], ACT.Copy, scale=0.5)
+        nc.scalar.activation(sign3[:], gain[:], ACT.Sign)
+        nc.scalar.activation(top_factor[:], sign3[:], ACT.Copy, scale=1.5, bias=0.5)
+        nc.scalar.activation(low_factor[:], sign3[:], ACT.Copy, scale=-1.5, bias=0.5)
         ident = held.tile([P, P], F32, name="ident")
         make_identity(nc, ident[:])
 
@@ -137,17 +137,21 @@ def tile_picked_hcandrangehopd_none_p_kernel(tc, x_words, x_scales, w1, gs, offs
         s_banks = [psum.tile([P, S], F32, name=f"s_bank{t}", tag=f"bank{4 + t}") for t in range(PACK)]
         s_win = [held.tile([P, S], F32, name=f"s_win{t}") for t in range(PACK)]
         s_plain = [held.tile([P, S], F32, name=f"s_plain{t}") for t in range(PACK)]
-        z_bf = [held.tile([P, b - a, PACK], BF16, name=f"z_bf{i}", align_bytes=64) for i, (a, b) in enumerate(PIECES)]
+        z_bf = [held.tile([P, b - a, PACK], BF16, name=f"z_bf{h}", tag=f"z_bf{h}", align_bytes=64) for h, (a, b) in enumerate(HALVES)]
         z_rows = held.tile([P, PACK, P], F32, name="z_rows")
         sums = [psum.tile([P, PACK, P], F32, name=f"sum{blk}", tag=f"bank{blk}") for blk in range(3)]
         units = [(i, t0, t0 + 2) for i in range(len(PIECES)) for t0 in (0, 2)]
         last = len(PIECES) - 1
         state = {}
+        behind_tag = {(units[2], "low_s"): "turned0", (units[2], "top_s"): "turned1", (units[5], "da"): "z_bf0"}
 
         def fresh(u, name):
             i, t0, t1 = u
             a, b = PIECES[i]
-            state[u, name] = work.tile([P, t1 - t0, b - a], F32, name=name)
+            if (u, name) in behind_tag:
+                state[u, name] = held.tile([P, t1 - t0, b - a], F32, name=name, tag=behind_tag[u, name], align_bytes=64)
+            else:
+                state[u, name] = work.tile([P, t1 - t0, b - a], F32, name=name)
             return state[u, name]
 
         def fetches(u):
@@ -160,16 +164,15 @@ def tile_picked_hcandrangehopd_none_p_kernel(tc, x_words, x_scales, w1, gs, offs
 
             return [partial(fetch, d, lst, t) for t in range(t0, t1) for d, lst in ((da, n1_l), (db, n2_l))]
 
-        def turn_back(i, blk):
-            a, b = PIECES[i]
-            turned = work.tile([P, 2, P, 2], BF16, name="turned")
+        def turn_back(blk):
+            turned = held.tile([P, 2, P, 2], BF16, name=f"turned{blk}", tag=f"turned{blk}", align_bytes=64)
             nc.scalar.copy(turned[:], sums[blk][:].rearrange("j (u e) p -> j u p e", e=2))
             words = turned[:].rearrange("j u p e -> j u (p e)").bitcast(F32)
             back = psum.tile([P, 2, P], F32, name="back", tag="bank3")
             for u in range(2):
                 nc.tensor.transpose(back[:, u, :], words[:, u, :], ident[:])
-            c0 = blk * P - a
-            dst = z_bf[i][:, c0 : c0 + P, :].rearrange("p c t -> p (c t)").bitcast(F32).rearrange("p (c u) -> p c u", u=2)
+            c0 = blk % 2 * P
+            dst = z_bf[blk // 2][:, c0 : c0 + P, :].rearrange("p c t -> p (c t)").bitcast(F32).rearrange("p (c u) -> p c u", u=2)
             nc.scalar.copy(dst, back[:].rearrange("p u c -> p c u"))
 
         def combines(u):
@@ -194,7 +197,7 @@ def tile_picked_hcandrangehopd_none_p_kernel(tc, x_words, x_scales, w1, gs, offs
                             nc.tensor.matmul(sums[blk][:, t, :], term, ident[:], start=k == 0, stop=k == 2, is_transpose=True)
                 if t1 == PACK:
                     for blk in range(a // P, b // P):
-                        turn_back(i, blk)
+                        turn_back(blk)
 
             def low_part():
                 part = fresh(u, "part")
@@ -207,20 +210,19 @@ def tile_picked_hcandrangehopd_none_p_kernel(tc, x_words, x_scales, w1, gs, offs
 
             return [extremes, low_part, top_part] if i == last else [extremes, by_tensor]
 
-        def score(i):
-            a, b = PIECES[i]
-            nc.vector.quantize_mx(out=z_codes[:, a:b].bitcast(FP8X4), scales=z_plane[:, a:b], in_=z_bf[i][:].rearrange("p c t -> p (c t)"))
+        def score(h):
+            a, b = HALVES[h]
+            nc.vector.quantize_mx(out=z_codes[:, a:b].bitcast(FP8X4), scales=z_plane[:, a:b], in_=z_bf[h][:].rearrange("p c t -> p (c t)"))
             for t in range(PACK):
                 cols = slice(t * P, (t + 1) * P)
                 nc.tensor.matmul_mx(out=s_banks[t][:, a:b], lhsT=c_codes[:, cols].bitcast(FP8X4), lhsT_scale=c_plane[:, cols],
                                     rhs=z_codes[:, a:b].bitcast(FP8X4), rhs_scale=z_plane[:, a:b], start=True, stop=True)
                 nc.scalar.activation(s_win[t][:, a:b], s_banks[t][:, a:b], ACT.Copy, scale=0.0625)
-                if i > 0:
+                if h == 1:
                     nc.scalar.activation(s_plain[t][:, a:b], s_banks[t][:, a:b], ACT.Copy, scale=0.0625)
                 else:
                     nc.sync.dma_start(s_plain[t][:, a:b], s_win[t][:, a:b])
 
-        score_after = {4: 0, 5: 1}
         for n in range(len(units) + 1):
             ahead = fetches(units[n]) if n < len(units) else []
             behind = combines(units[n - 1]) if n >= 1 else []
@@ -229,13 +231,13 @@ def tile_picked_hcandrangehopd_none_p_kernel(tc, x_words, x_scales, w1, gs, offs
                     ahead[k]()
                 if k < len(behind):
                     behind[k]()
-            if n in score_after:
-                score(score_after[n])
+            if n == 4:
+                score(0)
         nc.vector.tensor_copy(
-            z_bf[last][:].rearrange("p (c i) t -> p c t i", i=4),
+            z_bf[1][:, P : 2 * P, :].rearrange("p (c i) t -> p c t i", i=4),
             z_rows[:].rearrange("p t (c i) -> p c t i", i=4),
         )
-        score(last)
+        score(1)
 
         out_rows = out.rearrange("(a t b) j -> t a b j", t=PACK, b=8)
         gates = {}

from contextlib import ExitStack
from functools import partial

import concourse.mybir as mybir
from concourse.masks import make_identity

K, T, S, H, C = 512, 2048, 512, 512, 512
FLOPS = 2 * K * H * S + 2 * K * C * S

F32 = mybir.dt.float32
BF16 = mybir.dt.bfloat16
I32 = mybir.dt.int32
U32 = mybir.dt.uint32
U16 = mybir.dt.uint16
U8 = mybir.dt.uint8
FP8X4 = mybir.dt.float8_e4m3fn_x4
ALU = mybir.AluOpType
ACT = mybir.ActivationFunctionType

P = 128
PACK = 4
PIECES = ((0, 256), (256, 384), (384, 512))
HALVES = ((0, 256), (256, 512))


def tile_picked_hcandrangehopd_none_p_kernel(tc, x_words, x_scales, w1, gs, offs, n1, n2, cand, n3, n4, out):
    nc = tc.nc
    with ExitStack() as ctx:
        held = ctx.enter_context(tc.tile_pool(name="held", bufs=1))
        work = ctx.enter_context(tc.tile_pool(name="work", bufs=3))
        psum = ctx.enter_context(tc.psum_pool(name="psum", bufs=1))

        def load_list(name, src):
            lst = held.tile([P, S // 16], U16, name=name)
            nc.sync.dma_start(lst[:], src)
            return lst

        def entries(lst, a, b):
            return lst[:, a // 16 : b // 16]

        warm_in = held.tile([P, 1], F32, name="warm_in")
        warm_out = held.tile([P, 1], F32, name="warm_out")
        nc.gpsimd.memset(warm_in[:], 0.0)
        nc.scalar.activation(warm_out[:], warm_in[:], ACT.Sigmoid)

        offs_l = load_list("offs_l", offs)
        table_scales = held.tile([P, T], U8, name="table_scales", align_bytes=64)
        nc.sync.dma_start(table_scales[:].bitcast(I32), x_scales[0].bitcast(I32).unsqueeze(1).broadcast_to([16, 8, T // 4]))
        cand_l = load_list("cand_l", cand)
        n1_l = load_list("n1_l", n1)
        n2_l = load_list("n2_l", n2)
        table_words = held.tile([P, T], U32, name="table_words", align_bytes=64)
        words_src = x_words[0].rearrange("p c r -> p (c r)").bitcast(I32)
        for h in range(2):
            cols = slice(h * T // 2, (h + 1) * T // 2)
            nc.sync.dma_start(table_words[:].bitcast(I32)[:, cols], words_src[:, cols])
        w_raw = []
        for h, (a, b) in enumerate(HALVES):
            half = held.tile([P, PACK, b - a], F32, name=f"w_raw{h}")
            nc.sync.dma_start(half[:], w1.rearrange("(p j) c -> p j c", j=PACK)[:, :, a:b])
            w_raw.append(half)
        n3_l = load_list("n3_l", n3)
        n4_l = load_list("n4_l", n4)
        gain = held.tile([P, PACK], F32, name="gain")
        nc.gpsimd.dma_start(gain[:], gs.rearrange("(p t) o -> p (t o)", t=PACK))

        gain_half = held.tile([P, PACK], F32, name="gain_half")
        sign3 = held.tile([P, PACK], F32, name="sign3")
        top_factor = held.tile([P, PACK], F32, name="top_factor")
        low_factor = held.tile([P, PACK], F32, name="low_factor")
        nc.scalar.activation(gain_half[:], gain[:], ACT.Copy, scale=0.5)
        nc.scalar.activation(sign3[:], gain[:], ACT.Sign)
        nc.scalar.activation(top_factor[:], sign3[:], ACT.Copy, scale=1.5, bias=0.5)
        nc.scalar.activation(low_factor[:], sign3[:], ACT.Copy, scale=-1.5, bias=0.5)
        ident = held.tile([P, P], F32, name="ident")
        make_identity(nc, ident[:])

        x_plane = held.tile([P, S], U8, name="x_plane", align_bytes=64)
        c_plane = held.tile([P, C], U8, name="c_plane", align_bytes=64)
        nc.vector.memset(x_plane[:].bitcast(I32), 0)
        nc.vector.memset(c_plane[:].bitcast(I32), 0)

        x_bytes = held.tile([P, S], U8, name="x_bytes", align_bytes=64)
        nc.vector.tensor_copy(x_bytes[:], table_scales[:].indirect(offs_l[:]))
        for r in range(4):
            nc.scalar.dma_start(x_plane[r:P:32, :].bitcast(I32), x_bytes[8 * r : P : 32, :].bitcast(I32))
        c_bytes = held.tile([P, C], U8, name="c_bytes", align_bytes=64)
        nc.vector.tensor_copy(c_bytes[:], table_scales[:].indirect(cand_l[:]))

        c_bytes_dealt = held.tile([P, C], U8, name="c_bytes_dealt", align_bytes=64)
        nc.vector.tensor_copy(
            c_bytes_dealt[:].bitcast(I32).rearrange("p (t a b) -> p t a b", t=PACK, b=2),
            c_bytes[:].bitcast(I32).rearrange("p (a t b) -> p t a b", t=PACK, b=2),
        )
        for r in range(4):
            nc.sync.dma_start(c_plane[r:P:32, :].bitcast(I32), c_bytes_dealt[8 * r : P : 32, :].bitcast(I32))

        x_codes = held.tile([P, S], U32, name="x_codes", align_bytes=64)
        nc.vector.tensor_copy(x_codes[:], table_words[:].indirect(offs_l[:]))

        w_first = held.tile([P, P * PACK], BF16, name="w_first", tag="w_first", align_bytes=64)
        w_rest = held.tile([P, (H - P) * PACK], BF16, name="w_rest", align_bytes=64)
        first_view = w_first[:].rearrange("p (m j) -> p m j", j=PACK)
        rest_view = w_rest[:].rearrange("p (t m j) -> p m j t", t=PACK - 1, j=PACK)
        w_src = [w_raw[h][:].rearrange("p j (m t) -> p m j t", t=PACK) for h in range(2)]
        nc.scalar.copy(first_view[:, 0:64], w_src[0][:, :, :, 0])
        nc.scalar.copy(rest_view[:, 0:64], w_src[0][:, :, :, 1:4])
        nc.vector.tensor_copy(first_view[:, 64:128], w_src[1][:, :, :, 0])
        nc.scalar.copy(rest_view[:, 64:128], w_src[1][:, :, :, 1:4])
        w_codes = held.tile([P, H], U32, name="w_codes", align_bytes=64)
        w_plane = held.tile([P, H], U8, name="w_plane", align_bytes=64)
        nc.vector.quantize_mx(out=w_codes[:, 0:P].bitcast(FP8X4), scales=w_plane[:, 0:P], in_=w_first[:])
        for a, b in ((128, 256), (256, 512)):
            nc.vector.quantize_mx(out=w_codes[:, a:b].bitcast(FP8X4), scales=w_plane[:, a:b], in_=w_rest[:, (a - P) * PACK : (b - P) * PACK])

        c_words = held.tile([P, C], U32, name="c_words", tag="w_first", align_bytes=64)
        nc.vector.tensor_copy(c_words[:], table_words[:].indirect(cand_l[:]))
        c_codes = held.tile([P, C], U32, name="c_codes", align_bytes=64)
        nc.vector.tensor_copy(
            c_codes[:].rearrange("p (t a b) -> p t a b", t=PACK, b=8),
            c_words[:].rearrange("p (a t b) -> p t a b", t=PACK, b=8),
        )

        y_win = [held.tile([P, S], F32, name=f"y_win{t}") for t in range(PACK)]
        y_plain = held.tile([P, PACK, S], F32, name="y_plain")
        for t in range(PACK):
            cols = slice(t * P, (t + 1) * P)
            bank = psum.tile([P, S], F32, name=f"y_bank{t}", tag=f"bank{t}")
            nc.tensor.matmul_mx(out=bank[:], lhsT=w_codes[:, cols].bitcast(FP8X4), lhsT_scale=w_plane[:, cols],
                                rhs=x_codes[:].bitcast(FP8X4), rhs_scale=x_plane[:], start=True, stop=True)
            nc.scalar.activation(y_win[t][:], bank[:], ACT.Copy, scale=gain_half[:, t : t + 1])
            nc.scalar.activation(y_plain[:, t, 0:256], bank[:, 0:256], ACT.Copy, scale=gain_half[:, t : t + 1])
            nc.sync.dma_start(y_plain[:, t, 256:512], y_win[t][:, 256:512])

        z_codes = held.tile([P, S], U32, name="z_codes", align_bytes=64)
        z_plane = held.tile([P, S], U8, name="z_plane", align_bytes=64)
        s_banks = [psum.tile([P, S], F32, name=f"s_bank{t}", tag=f"bank{4 + t}") for t in range(PACK)]
        s_win = [held.tile([P, S], F32, name=f"s_win{t}") for t in range(PACK)]
        s_plain = [held.tile([P, S], F32, name=f"s_plain{t}") for t in range(PACK)]
        z_bf = [held.tile([P, b - a, PACK], BF16, name=f"z_bf{h}", tag=f"z_bf{h}", align_bytes=64) for h, (a, b) in enumerate(HALVES)]
        z_rows = held.tile([P, PACK, P], F32, name="z_rows")
        sums = [psum.tile([P, PACK, P], F32, name=f"sum{blk}", tag=f"bank{blk}") for blk in range(3)]
        units = [(i, t0, t0 + 2) for i in range(len(PIECES)) for t0 in (0, 2)]
        last = len(PIECES) - 1
        state = {}
        behind_tag = {(units[2], "low_s"): "turned0", (units[2], "top_s"): "turned1", (units[5], "da"): "z_bf0"}

        def fresh(u, name):
            i, t0, t1 = u
            a, b = PIECES[i]
            if (u, name) in behind_tag:
                state[u, name] = held.tile([P, t1 - t0, b - a], F32, name=name, tag=behind_tag[u, name], align_bytes=64)
            else:
                state[u, name] = work.tile([P, t1 - t0, b - a], F32, name=name)
            return state[u, name]

        def fetches(u):
            i, t0, t1 = u
            a, b = PIECES[i]
            da, db = fresh(u, "da"), fresh(u, "db")

            def fetch(d, lst, t):
                nc.vector.tensor_tensor(d[:, t - t0, :], y_win[t][:].indirect(entries(lst, a, b)), y_plain[:, t, a:b], ALU.subtract)

            return [partial(fetch, d, lst, t) for t in range(t0, t1) for d, lst in ((da, n1_l), (db, n2_l))]

        def turn_back(blk):
            turned = held.tile([P, 2, P, 2], BF16, name=f"turned{blk}", tag=f"turned{blk}", align_bytes=64)
            nc.scalar.copy(turned[:], sums[blk][:].rearrange("j (u e) p -> j u p e", e=2))
            words = turned[:].rearrange("j u p e -> j u (p e)").bitcast(F32)
            back = psum.tile([P, 2, P], F32, name="back", tag="bank3")
            for u in range(2):
                nc.tensor.transpose(back[:, u, :], words[:, u, :], ident[:])
            c0 = blk % 2 * P
            dst = z_bf[blk // 2][:, c0 : c0 + P, :].rearrange("p c t -> p (c t)").bitcast(F32).rearrange("p (c u) -> p c u", u=2)
            nc.scalar.copy(dst, back[:].rearrange("p u c -> p c u"))

        def combines(u):
            i, t0, t1 = u
            a, b = PIECES[i]

            def extremes():
                da, db = state[u, "da"], state[u, "db"]
                nc.vector.scalar_tensor_tensor(fresh(u, "low")[:], da[:], 0.0, db[:], ALU.min, ALU.min)
                nc.vector.scalar_tensor_tensor(fresh(u, "top")[:], da[:], 0.0, db[:], ALU.max, ALU.max)

            def by_tensor():
                low_s, top_s = fresh(u, "low_s"), fresh(u, "top_s")
                for t in range(t0, t1):
                    q = t - t0
                    nc.scalar.activation(low_s[:, q, :], state[u, "low"][:, q, :], ACT.Copy, scale=low_factor[:, t : t + 1])
                    nc.scalar.activation(top_s[:, q, :], state[u, "top"][:, q, :], ACT.Copy, scale=top_factor[:, t : t + 1])
                    for blk in range(a // P, b // P):
                        c0 = blk * P - a
                        terms = (y_plain[:, t, blk * P : (blk + 1) * P], low_s[:, q, c0 : c0 + P], top_s[:, q, c0 : c0 + P])
                        for k, term in enumerate(terms):
                            nc.tensor.matmul(sums[blk][:, t, :], term, ident[:], start=k == 0, stop=k == 2, is_transpose=True)
                if t1 == PACK:
                    for blk in range(a // P, b // P):
                        turn_back(blk)

            def low_part():
                part = fresh(u, "part")
                for t in range(t0, t1):
                    nc.vector.scalar_tensor_tensor(part[:, t - t0, :], state[u, "low"][:, t - t0, :], low_factor[:, t : t + 1], y_plain[:, t, a:b], ALU.mult, ALU.add)

            def top_part():
                for t in range(t0, t1):
                    nc.vector.scalar_tensor_tensor(z_rows[:, t, :], state[u, "top"][:, t - t0, :], top_factor[:, t : t + 1], state[u, "part"][:, t - t0, :], ALU.mult, ALU.add)

            return [extremes, low_part, top_part] if i == last else [extremes, by_tensor]

        def score(h):
            a, b = HALVES[h]
            nc.vector.quantize_mx(out=z_codes[:, a:b].bitcast(FP8X4), scales=z_plane[:, a:b], in_=z_bf[h][:].rearrange("p c t -> p (c t)"))
            for t in range(PACK):
                cols = slice(t * P, (t + 1) * P)
                nc.tensor.matmul_mx(out=s_banks[t][:, a:b], lhsT=c_codes[:, cols].bitcast(FP8X4), lhsT_scale=c_plane[:, cols],
                                    rhs=z_codes[:, a:b].bitcast(FP8X4), rhs_scale=z_plane[:, a:b], start=True, stop=True)
                nc.scalar.activation(s_win[t][:, a:b], s_banks[t][:, a:b], ACT.Copy, scale=0.0625)
                if h == 1:
                    nc.scalar.activation(s_plain[t][:, a:b], s_banks[t][:, a:b], ACT.Copy, scale=0.0625)
                else:
                    nc.sync.dma_start(s_plain[t][:, a:b], s_win[t][:, a:b])

        for n in range(len(units) + 1):
            ahead = fetches(units[n]) if n < len(units) else []
            behind = combines(units[n - 1]) if n >= 1 else []
            for k in range(max(len(ahead), len(behind))):
                if k < len(ahead):
                    ahead[k]()
                if k < len(behind):
                    behind[k]()
            if n == 4:
                score(0)
        nc.vector.tensor_copy(
            z_bf[1][:, P : 2 * P, :].rearrange("p (c i) t -> p c t i", i=4),
            z_rows[:].rearrange("p t (c i) -> p c t i", i=4),
        )
        score(1)

        out_rows = out.rearrange("(a t b) j -> t a b j", t=PACK, b=8)
        gates = {}

        last_parts = ((0, 256), (256, 384), (384, 512))

        def step(t):
            st = work.tile([P, S], F32, name="st", bufs=4)
            for a, b in HALVES:
                nc.vector.tensor_tensor(st[:, a:b], s_win[t][:].indirect(entries(n3_l, a, b)), s_plain[t][:, a:b], ALU.subtract)
            gates[t] = work.tile([P, S], F32, name="gate", bufs=4)
            for a, b in last_parts if t == PACK - 1 else HALVES:
                nc.scalar.activation(gates[t][:, a:b], st[:].indirect(entries(n4_l, a, b)), ACT.Sigmoid)

        def emit(t):
            for a, b in last_parts if t == PACK - 1 else ((0, S),):
                res = work.tile([P, b - a], F32, name="res", bufs=6)
                nc.vector.tensor_tensor(res[:], gates[t][:, a:b], s_plain[t][:, a:b], ALU.mult)
                nc.sync.dma_start(out_rows[t][:, :, a:b], res[:])

        for t in range(PACK + 2):
            if t < PACK:
                step(t)
            if t >= 2:
                emit(t - 2)
